import numpy as np
import ml_dtypes


def mxq(x, axis, fmt="e4m3"):
    dtype, down = {"e4m3": (ml_dtypes.float8_e4m3fn, 7), "e5m2": (ml_dtypes.float8_e5m2, 14)}[fmt]
    v = np.moveaxis(np.asarray(x, np.float32).astype(ml_dtypes.bfloat16).astype(np.float64), axis, -1)
    blocks = v.reshape(v.shape[:-1] + (-1, 32))
    amax = np.abs(blocks).max(-1, keepdims=True)
    byte = np.maximum(np.where(amax > 0, np.frexp(amax)[1] - 1 + 127, 0) - down, 1)
    scale = np.exp2(byte - 127.0)
    codes = (blocks / scale).astype(np.float32).astype(dtype).astype(np.float64)
    return np.moveaxis((codes * scale).reshape(v.shape), -1, axis)


WIDE = False


def mx_kscale(k):
    if not WIDE:
        return np.ones(k)
    levels = np.array([10, -10, 5, -5, 0])
    if k % 512:
        return np.exp2(np.random.permutation(np.resize(levels, k // 32))).repeat(32)
    a = np.empty((k // 512, 16))
    for p in range(k // 512):
        a[p, :8] = np.random.permutation(np.resize(levels, 8))
        for g in range(8):
            far = levels[np.abs(levels - a[p, g]) >= 10]
            a[p, g + 8] = far[np.random.randint(len(far))]
    return np.exp2(a.ravel()).repeat(32)


def f64(x):
    return np.asarray(x).astype(np.float64)


def striped(idx):
    return np.tile(idx.reshape(-1, 16).T, (8, 1)).astype(np.uint16)


def unstriped(offs):
    return offs[:16].T.reshape(-1).astype(np.int64)


E2M1 = np.array([0.0, 0.5, 1.0, 1.5, 2.0, 3.0, 4.0, 6.0, -0.0, -0.5, -1.0, -1.5, -2.0, -3.0, -4.0, -6.0])


def pack_weight(w, fmt):
    k, n = w.shape
    w = f64(np.asarray(w, np.float32).astype(ml_dtypes.bfloat16)).reshape(k // 32, 32, n)
    amax = np.abs(w).max(1)
    if fmt == "e4m3":
        byte = np.frexp(amax)[1] - 1 + 127 - 7
    else:
        mant, ex = np.frexp(amax / 6.0)
        byte = np.where(mant > 0.5, ex, ex - 1) + 127
    byte = np.clip(np.where(amax > 0, byte, 1), 1, 254)
    scaled = (w * np.exp2(127.0 - byte)[:, None, :]).reshape(k, n).astype(np.float32)
    by_word = np.ascontiguousarray(scaled.reshape(k // 512, 128, 4, n).transpose(0, 1, 3, 2))
    if fmt == "e4m3":
        words = by_word.astype(ml_dtypes.float8_e4m3fn).view(np.uint8)
    else:
        c = by_word.astype(ml_dtypes.float4_e2m1fn).view(np.uint8) & 0xF
        words = (c[..., 0::2] | (c[..., 1::2] << 4)).reshape(k // 512, 128, 2 * n)
    return np.ascontiguousarray(words), np.ascontiguousarray(byte.astype(np.uint8).reshape(k // 512, 16, n))


def unpack_weight(words, scales, fmt):
    g, _, n = scales.shape
    words = np.ascontiguousarray(words).reshape(g, 128, n, -1)
    if fmt == "e4m3":
        vals = words.view(ml_dtypes.float8_e4m3fn).astype(np.float64)
    else:
        nib = np.empty((g, 128, n, 4), np.uint8)
        nib[..., 0::2] = words & 0xF
        nib[..., 1::2] = words >> 4
        vals = E2M1[nib]
    vals = vals * np.repeat(np.exp2(scales.astype(np.float64) - 127.0), 8, axis=1)[..., None]
    return vals.transpose(0, 1, 3, 2).reshape(g * 512, n)


K, M, T, S = 1024, 128, 2048, 1024


def setup_inputs():
    n = np.random.standard_normal
    s = mx_kscale(K)[:, None]
    u = mx_kscale(512)[:, None]
    v = pack_weight(n((K, T)) * s, "e4m3")
    p_w2 = pack_weight(1.4 * n((512, M)) / np.sqrt(512) / u, "e2m1")
    return {
        "tab_words": v[0],
        "tab_scales": v[1],
        "w1": (n((K, 512)) / np.sqrt(K) / s * u.T).astype(np.float32),
        "w2_words": p_w2[0],
        "w2_scales": p_w2[1],
        "gT": n((M, T)).astype(np.float32),
        "offs": striped(np.random.permutation(T)[:S]),
    }


def reference(tab_words, tab_scales, w1, w2_words, w2_scales, gT, offs):
    tab_ = unpack_weight(tab_words, tab_scales, "e4m3")[:, unstriped(offs)]
    w1_ = mxq(f64(w1), 0, "e4m3")
    w2_ = unpack_weight(w2_words, w2_scales, "e2m1")
    h_ = mxq(np.maximum(w1_.T @ tab_, 0.0), 0, "e4m3")
    y = w2_.T @ h_
    return (y) * f64(gT)[:, unstriped(offs)]

@@ -1,0 +1,171 @@
+from contextlib import ExitStack
+
+import concourse.mybir as mybir
+
+K, M, T, S, H = 1024, 128, 2048, 1024, 512
+FLOPS = 2 * K * H * S + 2 * H * M * S
+
+F32 = mybir.dt.float32
+BF16 = mybir.dt.bfloat16
+I32 = mybir.dt.int32
+U32 = mybir.dt.uint32
+U16 = mybir.dt.uint16
+U8 = mybir.dt.uint8
+FP8X4 = mybir.dt.float8_e4m3fn_x4
+FP4X4 = mybir.dt.float4_e2m1fn_x4
+RELU = mybir.ActivationFunctionType.Relu
+MULT = mybir.AluOpType.mult
+
+P = 128
+BANK_TOKENS = 128
+CHUNKS = [(0, 2), (2, 4), (4, 6), (6, 7), (7, 8)]
+RELU_ON_VECTOR = (5,)
+SCALAR_COLUMNS = 48
+
+
+def tile_list_tabgate_none_kernel(
+    tc, tab_words, tab_scales, w1, w2_words, w2_scales, gT, offs, out
+):
+    nc = tc.nc
+    with ExitStack() as ctx:
+        keep = ctx.enter_context(tc.tile_pool(name="keep", bufs=1))
+        psum = ctx.enter_context(tc.psum_pool(name="psum", bufs=1))
+
+        offsets = keep.tile([P, S // 16], U16, name="offsets")
+        table = [keep.tile([P, T], I32, name="table%d" % a, align_bytes=64) for a in range(2)]
+        table_scales = keep.tile([P, T // 4], I32, name="table_scales", align_bytes=64)
+        gates = keep.tile([P, T], F32, name="gates", align_bytes=64)
+        w1_raw = [keep.tile([P, 4, H], F32, name="w1_raw%d" % a, align_bytes=64) for a in range(2)]
+        w1_bf = [keep.tile([P, 4, P, 4], BF16, name="w1_bf%d" % a, align_bytes=64) for a in range(2)]
+        w1_codes = [keep.tile([P, H], U32, name="w1_codes%d" % a, align_bytes=64) for a in range(2)]
+        w1_sc = [keep.tile([P, H], U8, name="w1_sc%d" % a, align_bytes=64) for a in range(2)]
+        w2_codes = keep.tile([P, 2 * M], U8, name="w2_codes", align_bytes=64)
+        w2_sc = keep.tile([P, M // 4], I32, name="w2_sc", align_bytes=64)
+        v_codes = [keep.tile([P, S], U32, name="v_codes%d" % a, align_bytes=64) for a in range(2)]
+        v_sc = keep.tile([P, S], U8, name="v_sc", align_bytes=64)
+        h_bf = keep.tile([P, S, 4], BF16, name="h_bf", align_bytes=64)
+        h_codes = keep.tile([P, S], U32, name="h_codes", align_bytes=64)
+        h_sc = keep.tile([P, S], U8, name="h_sc", align_bytes=64)
+        y = keep.tile([P, S], F32, name="y", align_bytes=64)
+        result = keep.tile([P, S], F32, name="result", align_bytes=64)
+        warm = keep.tile([P, 8], F32, name="warm")
+
+        nc.vector.memset(table_scales[:], 0)
+        nc.vector.memset(w2_sc[:], 0)
+        nc.vector.memset(warm[:], 0.0)
+        nc.scalar.activation(warm[:, 0:1], warm[:, 1:2], RELU)
+
+        def load_table(a):
+            nc.sync.dma_start(table[a][:], tab_words[a].rearrange("p t i -> p (t i)").bitcast(I32))
+
+        def load_w1(a):
+            nc.sync.dma_start(w1_raw[a][:], w1[512 * a : 512 * (a + 1), :].rearrange("(p j) c -> p j c", j=4))
+
+        load_w1(0)
+        nc.sync.dma_start(offsets[:], offs)
+        for q in range(4):
+            nc.sync.dma_start(
+                table_scales[32 * q : 32 * q + 8, :], tab_scales[:, 4 * q : 4 * q + 4, :].bitcast(I32)
+            )
+        load_table(0)
+        load_w1(1)
+        load_table(1)
+        nc.sync.dma_start(gates[:], gT)
+        nc.sync.dma_start(w2_codes[:].bitcast(I32), w2_words[0].bitcast(I32))
+        for q in range(4):
+            nc.sync.dma_start(
+                w2_sc[32 * q : 32 * q + 4, :], w2_scales[0, 4 * q : 4 * q + 4, :].bitcast(I32)
+            )
+
+        def listed(lo, hi):
+            return offsets[:, lo // 16 : hi // 16]
+
+        def gather_words(a, lo, hi):
+            nc.vector.tensor_copy(v_codes[a][:, lo:hi], table[a][:].bitcast(U32).indirect(listed(lo, hi)))
+
+        def gather_scales(lo, hi):
+            nc.vector.tensor_copy(v_sc[:, lo:hi], table_scales[:].bitcast(U8).indirect(listed(lo, hi)))
+
+        def cast_w1(a):
+            dst = w1_bf[a][:].rearrange("p t m j -> p m t j")
+            src = w1_raw[a][:].rearrange("p j (m t) -> p m t j", t=4)
+            nc.scalar.copy(dst[:, :SCALAR_COLUMNS], src[:, :SCALAR_COLUMNS])
+            nc.vector.tensor_copy(dst[:, SCALAR_COLUMNS:], src[:, SCALAR_COLUMNS:])
+
+        def quantize_w1(a, t0, t1):
+            nc.vector.quantize_mx(
+                out=w1_codes[a][:, P * t0 : P * t1].bitcast(FP8X4),
+                scales=w1_sc[a][:, P * t0 : P * t1],
+                in_=w1_bf[a][:, t0:t1, :, :].rearrange("p t m j -> p (t m j)"),
+            )
+
+        banks = [psum.tile([P, 4, BANK_TOKENS], F32, name="bank%d" % b) for b in range(8)]
+
+        def first_layer(a, b):
+            cols = slice(BANK_TOKENS * b, BANK_TOKENS * (b + 1))
+            for t in range(4):
+                nc.tensor.matmul_mx(
+                    out=banks[b][:, t, :],
+                    lhsT=w1_codes[a][:, P * t : P * (t + 1)].bitcast(FP8X4),
+                    lhsT_scale=w1_sc[a][:, P * t : P * (t + 1)],
+                    rhs=v_codes[a][:, cols].bitcast(FP8X4),
+                    rhs_scale=v_sc[4 * a : P, cols],
+                    start=(a == 0 and t == 0),
+                    stop=(a == 1 and t == 3),
+                )
+
+        def relu(b):
+            cols = slice(BANK_TOKENS * b, BANK_TOKENS * (b + 1))
+            src = banks[b][:].rearrange("p t n -> p n t")
+            if b in RELU_ON_VECTOR:
+                nc.vector.tensor_scalar_max(h_bf[:, cols, :], src, 0.0)
+            else:
+                nc.scalar.activation(h_bf[:, cols, :], src, RELU)
+
+        def quantize_h(b0, b1):
+            cols = slice(BANK_TOKENS * b0, BANK_TOKENS * b1)
+            nc.vector.quantize_mx(
+                out=h_codes[:, cols].bitcast(FP8X4),
+                scales=h_sc[:, cols],
+                in_=h_bf[:, cols, :].rearrange("p n t -> p (n t)"),
+            )
+
+        def second_layer(b0, b1):
+            cols = slice(BANK_TOKENS * b0, BANK_TOKENS * b1)
+            acc = psum.tile([P, BANK_TOKENS * (b1 - b0)], F32, name="bank%d" % b0)
+            nc.tensor.matmul_mx(
+                out=acc[:],
+                lhsT=w2_codes[:].bitcast(FP4X4),
+                lhsT_scale=w2_sc[:].bitcast(U8),
+                rhs=h_codes[:, cols].bitcast(FP8X4),
+                rhs_scale=h_sc[:, cols],
+                start=True,
+                stop=True,
+            )
+            nc.scalar.copy(y[:, cols], acc[:])
+
+        def gate_and_store(b0, b1):
+            lo, hi = BANK_TOKENS * b0, BANK_TOKENS * b1
+            nc.vector.tensor_tensor(result[:, lo:hi], gates[:].indirect(listed(lo, hi)), y[:, lo:hi], MULT)
+            nc.sync.dma_start(out[:, lo:hi], result[:, lo:hi])
+
+        cast_w1(0)
+        gather_scales(0, S)
+        quantize_w1(0, 0, 4)
+        for c in range(4):
+            gather_words(0, 256 * c, 256 * (c + 1))
+            first_layer(0, 2 * c)
+            first_layer(0, 2 * c + 1)
+        cast_w1(1)
+        quantize_w1(1, 0, 4)
+        for c in range(4):
+            gather_words(1, 256 * c, 256 * (c + 1))
+        for i, chunk in enumerate(CHUNKS):
+            for b in range(*chunk):
+                first_layer(1, b)
+                relu(b)
+            quantize_h(*chunk)
+            second_layer(*chunk)
+            if i > 0:
+                gate_and_store(*CHUNKS[i - 1])
+        gate_and_store(*CHUNKS[-1])

@@ -19,8 +19,8 @@ MULT = mybir.AluOpType.mult
 P = 128
 BANK_TOKENS = 128
 CHUNKS = [(0, 2), (2, 4), (4, 6), (6, 7), (7, 8)]
-RELU_ON_VECTOR = (5,)
-SCALAR_COLUMNS = 48
+RELU_ON_VECTOR = (1, 3)
+W1_PIECES = (1, 2)
 
 
 def tile_list_tabgate_none_kernel(
@@ -35,7 +35,13 @@ def tile_list_tabgate_none_kernel(
         table = [keep.tile([P, T], I32, name="table%d" % a, align_bytes=64) for a in range(2)]
         table_scales = keep.tile([P, T // 4], I32, name="table_scales", align_bytes=64)
         gates = keep.tile([P, T], F32, name="gates", align_bytes=64)
-        w1_raw = [keep.tile([P, 4, H], F32, name="w1_raw%d" % a, align_bytes=64) for a in range(2)]
+        w1_raw = [
+            [
+                keep.tile([P, 4, H // W1_PIECES[a]], F32, name="w1_raw%d%d" % (a, u), align_bytes=64)
+                for u in range(W1_PIECES[a])
+            ]
+            for a in range(2)
+        ]
         w1_bf = [keep.tile([P, 4, P, 4], BF16, name="w1_bf%d" % a, align_bytes=64) for a in range(2)]
         w1_codes = [keep.tile([P, H], U32, name="w1_codes%d" % a, align_bytes=64) for a in range(2)]
         w1_sc = [keep.tile([P, H], U8, name="w1_sc%d" % a, align_bytes=64) for a in range(2)]
@@ -58,24 +64,28 @@ def tile_list_tabgate_none_kernel(
         def load_table(a):
             nc.sync.dma_start(table[a][:], tab_words[a].rearrange("p t i -> p (t i)").bitcast(I32))
 
-        def load_w1(a):
-            nc.sync.dma_start(w1_raw[a][:], w1[512 * a : 512 * (a + 1), :].rearrange("(p j) c -> p j c", j=4))
+        def load_w1(a, u):
+            rows = w1[512 * a : 512 * (a + 1), :].rearrange("(p j) c -> p j c", j=4)
+            nc.sync.dma_start(w1_raw[a][u][:], rows[:, :, H // W1_PIECES[a] * u : H // W1_PIECES[a] * (u + 1)])
 
-        load_w1(0)
+        first_rows = w1[0:512, :].rearrange("(p j) c -> p j c", j=4)
+        nc.sync.dma_start(w1_raw[0][0][:, 0:2, :], first_rows[:, 0:2, :])
         nc.sync.dma_start(offsets[:], offs)
         for q in range(4):
             nc.sync.dma_start(
                 table_scales[32 * q : 32 * q + 8, :], tab_scales[:, 4 * q : 4 * q + 4, :].bitcast(I32)
             )
+        nc.sync.dma_start(w1_raw[0][0][:, 2:4, :], first_rows[:, 2:4, :])
         load_table(0)
-        load_w1(1)
         load_table(1)
-        nc.sync.dma_start(gates[:], gT)
-        nc.sync.dma_start(w2_codes[:].bitcast(I32), w2_words[0].bitcast(I32))
+        for u in range(W1_PIECES[1]):
+            load_w1(1, u)
+        nc.gpsimd.dma_start(w2_codes[:].bitcast(I32), w2_words[0].bitcast(I32))
         for q in range(4):
-            nc.sync.dma_start(
+            nc.gpsimd.dma_start(
                 w2_sc[32 * q : 32 * q + 4, :], w2_scales[0, 4 * q : 4 * q + 4, :].bitcast(I32)
             )
+        nc.sync.dma_start(gates[:], gT)
 
         def listed(lo, hi):
             return offsets[:, lo // 16 : hi // 16]
@@ -86,11 +96,13 @@ def tile_list_tabgate_none_kernel(
         def gather_scales(lo, hi):
             nc.vector.tensor_copy(v_sc[:, lo:hi], table_scales[:].bitcast(U8).indirect(listed(lo, hi)))
 
-        def cast_w1(a):
-            dst = w1_bf[a][:].rearrange("p t m j -> p m t j")
-            src = w1_raw[a][:].rearrange("p j (m t) -> p m t j", t=4)
-            nc.scalar.copy(dst[:, :SCALAR_COLUMNS], src[:, :SCALAR_COLUMNS])
-            nc.vector.tensor_copy(dst[:, SCALAR_COLUMNS:], src[:, SCALAR_COLUMNS:])
+        def cast_w1(a, u, on_scalar):
+            width = P // W1_PIECES[a]
+            dst = w1_bf[a][:, :, width * u : width * (u + 1), :].rearrange("p t m j -> p m t j")
+            src = w1_raw[a][u][:].rearrange("p j (m t) -> p m t j", t=4)
+            nc.scalar.copy(dst[:, :on_scalar], src[:, :on_scalar])
+            if on_scalar < width:
+                nc.vector.tensor_copy(dst[:, on_scalar:], src[:, on_scalar:])
 
         def quantize_w1(a, t0, t1):
             nc.vector.quantize_mx(
@@ -149,19 +161,22 @@ def tile_list_tabgate_none_kernel(
             nc.vector.tensor_tensor(result[:, lo:hi], gates[:].indirect(listed(lo, hi)), y[:, lo:hi], MULT)
             nc.sync.dma_start(out[:, lo:hi], result[:, lo:hi])
 
-        cast_w1(0)
         gather_scales(0, S)
+        cast_w1(0, 0, 80)
         quantize_w1(0, 0, 4)
         for c in range(4):
             gather_words(0, 256 * c, 256 * (c + 1))
-            first_layer(0, 2 * c)
-            first_layer(0, 2 * c + 1)
-        cast_w1(1)
-        quantize_w1(1, 0, 4)
-        for c in range(4):
-            gather_words(1, 256 * c, 256 * (c + 1))
+        for b in range(4):
+            first_layer(0, b)
+        gather_words(1, 0, S)
+        cast_w1(1, 0, 64)
+        cast_w1(1, 1, 20)
+        for t in range(4):
+            quantize_w1(1, t, t + 1)
         for i, chunk in enumerate(CHUNKS):
             for b in range(*chunk):
+                if b >= 4:
+                    first_layer(0, b)
                 first_layer(1, b)
                 relu(b)
             quantize_h(*chunk)

@@ -20,7 +20,7 @@ P = 128
 BANK_TOKENS = 128
 CHUNKS = [(0, 2), (2, 4), (4, 6), (6, 7), (7, 8)]
 RELU_ON_VECTOR = (1, 3)
-W1_PIECES = (1, 2)
+W1_PIECES = (1, 1)
 
 
 def tile_list_tabgate_none_kernel(
@@ -69,22 +69,21 @@ def tile_list_tabgate_none_kernel(
             nc.sync.dma_start(w1_raw[a][u][:], rows[:, :, H // W1_PIECES[a] * u : H // W1_PIECES[a] * (u + 1)])
 
         first_rows = w1[0:512, :].rearrange("(p j) c -> p j c", j=4)
-        nc.sync.dma_start(w1_raw[0][0][:, 0:2, :], first_rows[:, 0:2, :])
+        nc.sync.dma_start(w1_raw[0][0][:, 0:1, :], first_rows[:, 0:1, :])
         nc.sync.dma_start(offsets[:], offs)
         for q in range(4):
             nc.sync.dma_start(
                 table_scales[32 * q : 32 * q + 8, :], tab_scales[:, 4 * q : 4 * q + 4, :].bitcast(I32)
             )
-        nc.sync.dma_start(w1_raw[0][0][:, 2:4, :], first_rows[:, 2:4, :])
         load_table(0)
-        load_table(1)
-        for u in range(W1_PIECES[1]):
-            load_w1(1, u)
-        nc.gpsimd.dma_start(w2_codes[:].bitcast(I32), w2_words[0].bitcast(I32))
+        nc.sync.dma_start(w1_raw[0][0][:, 1:4, :], first_rows[:, 1:4, :])
+        nc.sync.dma_start(w2_codes[:].bitcast(I32), w2_words[0].bitcast(I32))
         for q in range(4):
-            nc.gpsimd.dma_start(
+            nc.sync.dma_start(
                 w2_sc[32 * q : 32 * q + 4, :], w2_scales[0, 4 * q : 4 * q + 4, :].bitcast(I32)
             )
+        load_table(1)
+        load_w1(1, 0)
         nc.sync.dma_start(gates[:], gT)
 
         def listed(lo, hi):
@@ -162,21 +161,16 @@ def tile_list_tabgate_none_kernel(
             nc.sync.dma_start(out[:, lo:hi], result[:, lo:hi])
 
         gather_scales(0, S)
-        cast_w1(0, 0, 80)
+        gather_words(0, 0, S)
+        cast_w1(0, 0, 72)
         quantize_w1(0, 0, 4)
-        for c in range(4):
-            gather_words(0, 256 * c, 256 * (c + 1))
-        for b in range(4):
-            first_layer(0, b)
         gather_words(1, 0, S)
-        cast_w1(1, 0, 64)
-        cast_w1(1, 1, 20)
+        cast_w1(1, 0, 52)
         for t in range(4):
             quantize_w1(1, t, t + 1)
         for i, chunk in enumerate(CHUNKS):
             for b in range(*chunk):
-                if b >= 4:
-                    first_layer(0, b)
+                first_layer(0, b)
                 first_layer(1, b)
                 relu(b)
             quantize_h(*chunk)

@@ -19,7 +19,7 @@ MULT = mybir.AluOpType.mult
 P = 128
 BANK_TOKENS = 128
 CHUNKS = [(0, 2), (2, 4), (4, 6), (6, 7), (7, 8)]
-RELU_ON_VECTOR = (1, 3)
+RELU_ON_VECTOR = (5,)
 W1_PIECES = (1, 1)
 
 
@@ -75,15 +75,15 @@ def tile_list_tabgate_none_kernel(
             nc.sync.dma_start(
                 table_scales[32 * q : 32 * q + 8, :], tab_scales[:, 4 * q : 4 * q + 4, :].bitcast(I32)
             )
-        load_table(0)
         nc.sync.dma_start(w1_raw[0][0][:, 1:4, :], first_rows[:, 1:4, :])
+        load_table(0)
         nc.sync.dma_start(w2_codes[:].bitcast(I32), w2_words[0].bitcast(I32))
         for q in range(4):
             nc.sync.dma_start(
                 w2_sc[32 * q : 32 * q + 4, :], w2_scales[0, 4 * q : 4 * q + 4, :].bitcast(I32)
             )
-        load_table(1)
         load_w1(1, 0)
+        load_table(1)
         nc.sync.dma_start(gates[:], gT)
 
         def listed(lo, hi):
@@ -161,14 +161,16 @@ def tile_list_tabgate_none_kernel(
             nc.sync.dma_start(out[:, lo:hi], result[:, lo:hi])
 
         gather_scales(0, S)
-        gather_words(0, 0, S)
-        cast_w1(0, 0, 72)
+        cast_w1(0, 0, 32)
         quantize_w1(0, 0, 4)
-        gather_words(1, 0, S)
-        cast_w1(1, 0, 52)
-        for t in range(4):
-            quantize_w1(1, t, t + 1)
+        for c in range(4):
+            gather_words(0, 256 * c, 256 * (c + 1))
+        cast_w1(1, 0, 32)
+        quantize_w1(1, 0, 4)
+        gather_words(1, 0, 256)
         for i, chunk in enumerate(CHUNKS):
+            if i < 3:
+                gather_words(1, 256 * (i + 1), 256 * (i + 2))
             for b in range(*chunk):
                 first_layer(0, b)
                 first_layer(1, b)

@@ -97,8 +97,8 @@ def tile_list_tabgate_none_kernel(
 
         def cast_w1(a, u, on_scalar):
             width = P // W1_PIECES[a]
-            dst = w1_bf[a][:, :, width * u : width * (u + 1), :].rearrange("p t m j -> p m t j")
-            src = w1_raw[a][u][:].rearrange("p j (m t) -> p m t j", t=4)
+            dst = w1_bf[a][:, :, width * u : width * (u + 1), :].rearrange("p t m j -> p m j t")
+            src = w1_raw[a][u][:].rearrange("p j (m t) -> p m j t", t=4)
             nc.scalar.copy(dst[:, :on_scalar], src[:, :on_scalar])
             if on_scalar < width:
                 nc.vector.tensor_copy(dst[:, on_scalar:], src[:, on_scalar:])
@@ -161,11 +161,11 @@ def tile_list_tabgate_none_kernel(
             nc.sync.dma_start(out[:, lo:hi], result[:, lo:hi])
 
         gather_scales(0, S)
-        cast_w1(0, 0, 32)
+        cast_w1(0, 0, 56)
         quantize_w1(0, 0, 4)
         for c in range(4):
             gather_words(0, 256 * c, 256 * (c + 1))
-        cast_w1(1, 0, 32)
+        cast_w1(1, 0, 52)
         quantize_w1(1, 0, 4)
         gather_words(1, 0, 256)
         for i, chunk in enumerate(CHUNKS):

@@ -18,8 +18,7 @@ MULT = mybir.AluOpType.mult
 
 P = 128
 BANK_TOKENS = 128
-CHUNKS = [(0, 2), (2, 4), (4, 6), (6, 7), (7, 8)]
-RELU_ON_VECTOR = (5,)
+RELU_ON_VECTOR = (6, 7)
 W1_PIECES = (1, 1)
 
 
@@ -54,6 +53,7 @@ def tile_list_tabgate_none_kernel(
         h_sc = keep.tile([P, S], U8, name="h_sc", align_bytes=64)
         y = keep.tile([P, S], F32, name="y", align_bytes=64)
         result = keep.tile([P, S], F32, name="result", align_bytes=64)
+        picked = keep.tile([P, S], F32, name="picked", align_bytes=64)
         warm = keep.tile([P, 8], F32, name="warm")
 
         nc.vector.memset(table_scales[:], 0)
@@ -69,19 +69,30 @@ def tile_list_tabgate_none_kernel(
             nc.sync.dma_start(w1_raw[a][u][:], rows[:, :, H // W1_PIECES[a] * u : H // W1_PIECES[a] * (u + 1)])
 
         first_rows = w1[0:512, :].rearrange("(p j) c -> p j c", j=4)
-        nc.sync.dma_start(w1_raw[0][0][:, 0:1, :], first_rows[:, 0:1, :])
+
+        def load_scale_rows(i):
+            a, q = i % 2, 2 * (i // 2 % 2) + i // 4
+            first = 32 * q + 4 * a
+            nc.sync.dma_start(table_scales[first : first + 4, :], tab_scales[a, 4 * q : 4 * q + 4, :].bitcast(I32))
+
+        def load_scale_quadrant(q, queue):
+            queue.dma_start(table_scales[32 * q : 32 * q + 8, :], tab_scales[:, 4 * q : 4 * q + 4, :].bitcast(I32))
+
+        def load_w2(queue):
+            queue.dma_start(w2_codes[:].bitcast(I32), w2_words[0].bitcast(I32))
+            for q in range(4):
+                queue.dma_start(w2_sc[32 * q : 32 * q + 4, :], w2_scales[0, 4 * q : 4 * q + 4, :].bitcast(I32))
+
+        def load_first_rows(j0, j1):
+            nc.sync.dma_start(w1_raw[0][0][:, j0:j1, :], first_rows[:, j0:j1, :])
+
+        load_first_rows(0, 1)
         nc.sync.dma_start(offsets[:], offs)
         for q in range(4):
-            nc.sync.dma_start(
-                table_scales[32 * q : 32 * q + 8, :], tab_scales[:, 4 * q : 4 * q + 4, :].bitcast(I32)
-            )
-        nc.sync.dma_start(w1_raw[0][0][:, 1:4, :], first_rows[:, 1:4, :])
+            load_scale_quadrant(q, nc.sync)
+        load_first_rows(1, 4)
         load_table(0)
-        nc.sync.dma_start(w2_codes[:].bitcast(I32), w2_words[0].bitcast(I32))
-        for q in range(4):
-            nc.sync.dma_start(
-                w2_sc[32 * q : 32 * q + 4, :], w2_scales[0, 4 * q : 4 * q + 4, :].bitcast(I32)
-            )
+        load_w2(nc.sync)
         load_w1(1, 0)
         load_table(1)
         nc.sync.dma_start(gates[:], gT)
@@ -153,12 +164,28 @@ def tile_list_tabgate_none_kernel(
                 start=True,
                 stop=True,
             )
-            nc.scalar.copy(y[:, cols], acc[:])
+            return acc
 
         def gate_and_store(b0, b1):
             lo, hi = BANK_TOKENS * b0, BANK_TOKENS * b1
             nc.vector.tensor_tensor(result[:, lo:hi], gates[:].indirect(listed(lo, hi)), y[:, lo:hi], MULT)
             nc.sync.dma_start(out[:, lo:hi], result[:, lo:hi])
+
+        def copy_y(acc, b0, b1):
+            nc.scalar.copy(y[:, BANK_TOKENS * b0 : BANK_TOKENS * b1], acc[:])
+
+        def pick_gates(b0, b1):
+            lo, hi = BANK_TOKENS * b0, BANK_TOKENS * b1
+            nc.vector.tensor_copy(picked[:, lo:hi], gates[:].indirect(listed(lo, hi)))
+
+        def mul_and_store(acc, b0, b1):
+            lo, hi = BANK_TOKENS * b0, BANK_TOKENS * b1
+            nc.vector.tensor_tensor(result[:, lo:hi], acc[:], picked[:, lo:hi], MULT)
+            nc.sync.dma_start(out[:, lo:hi], result[:, lo:hi])
+
+        def both_passes(b):
+            first_layer(0, b)
+            first_layer(1, b)
 
         gather_scales(0, S)
         cast_w1(0, 0, 56)
@@ -167,16 +194,31 @@ def tile_list_tabgate_none_kernel(
             gather_words(0, 256 * c, 256 * (c + 1))
         cast_w1(1, 0, 52)
         quantize_w1(1, 0, 4)
-        gather_words(1, 0, 256)
-        for i, chunk in enumerate(CHUNKS):
-            if i < 3:
-                gather_words(1, 256 * (i + 1), 256 * (i + 2))
-            for b in range(*chunk):
-                first_layer(0, b)
-                first_layer(1, b)
-                relu(b)
-            quantize_h(*chunk)
-            second_layer(*chunk)
-            if i > 0:
-                gate_and_store(*CHUNKS[i - 1])
-        gate_and_store(*CHUNKS[-1])
+        for c in range(4):
+            gather_words(1, 256 * c, 256 * (c + 1))
+        for b in range(8):
+            both_passes(b)
+        relu(0)
+        relu(1)
+        pick_gates(4, 6)
+        quantize_h(0, 2)
+        acc0 = second_layer(0, 2)
+        relu(2)
+        relu(3)
+        relu(6)
+        relu(7)
+        quantize_h(2, 4)
+        copy_y(acc0, 0, 2)
+        acc1 = second_layer(2, 4)
+        relu(4)
+        relu(5)
+        gate_and_store(0, 2)
+        quantize_h(6, 8)
+        acc3 = second_layer(6, 8)
+        quantize_h(4, 6)
+        copy_y(acc1, 2, 4)
+        acc2 = second_layer(4, 6)
+        copy_y(acc3, 6, 8)
+        gate_and_store(2, 4)
+        gate_and_store(6, 8)
+        mul_and_store(acc2, 4, 6)

@@ -18,7 +18,7 @@ MULT = mybir.AluOpType.mult
 
 P = 128
 BANK_TOKENS = 128
-RELU_ON_VECTOR = (6, 7)
+RELU_ON_VECTOR = (3, 7)
 W1_PIECES = (1, 1)
 
 
@@ -180,7 +180,7 @@ def tile_list_tabgate_none_kernel(
 
         def mul_and_store(acc, b0, b1):
             lo, hi = BANK_TOKENS * b0, BANK_TOKENS * b1
-            nc.vector.tensor_tensor(result[:, lo:hi], acc[:], picked[:, lo:hi], MULT)
+            nc.vector.tensor_tensor(result[:, lo:hi], acc, picked[:, lo:hi], MULT)
             nc.sync.dma_start(out[:, lo:hi], result[:, lo:hi])
 
         def both_passes(b):
@@ -200,25 +200,26 @@ def tile_list_tabgate_none_kernel(
             both_passes(b)
         relu(0)
         relu(1)
-        pick_gates(4, 6)
+        relu(3)
+        pick_gates(6, 8)
         quantize_h(0, 2)
         acc0 = second_layer(0, 2)
         relu(2)
-        relu(3)
-        relu(6)
-        relu(7)
         quantize_h(2, 4)
-        copy_y(acc0, 0, 2)
         acc1 = second_layer(2, 4)
+        relu(7)
         relu(4)
+        copy_y(acc0, 0, 2)
         relu(5)
+        quantize_h(4, 6)
+        acc2 = second_layer(4, 6)
         gate_and_store(0, 2)
+        relu(6)
+        copy_y(acc1, 2, 4)
         quantize_h(6, 8)
         acc3 = second_layer(6, 8)
-        quantize_h(4, 6)
-        copy_y(acc1, 2, 4)
-        acc2 = second_layer(4, 6)
-        copy_y(acc3, 6, 8)
+        copy_y(acc2, 4, 6)
         gate_and_store(2, 4)
-        gate_and_store(6, 8)
-        mul_and_store(acc2, 4, 6)
+        gate_and_store(4, 6)
+        mul_and_store(acc3[:, 0:128], 6, 7)
+        mul_and_store(acc3[:, 128:256], 7, 8)

@@ -114,6 +114,14 @@ def tile_list_tabgate_none_kernel(
             if on_scalar < width:
                 nc.vector.tensor_copy(dst[:, on_scalar:], src[:, on_scalar:])
 
+        def cast_part(a, t0, t1, m0, m1, on_scalar):
+            dst = w1_bf[a][:, t0:t1, m0:m1, :].rearrange("p t m j -> p m j t")
+            src = w1_raw[a][0][:].rearrange("p j (m t) -> p m j t", t=4)[:, m0:m1, :, t0:t1]
+            if on_scalar:
+                nc.scalar.copy(dst, src)
+            else:
+                nc.vector.tensor_copy(dst, src)
+
         def quantize_w1(a, t0, t1):
             nc.vector.quantize_mx(
                 out=w1_codes[a][:, P * t0 : P * t1].bitcast(FP8X4),
@@ -190,10 +198,14 @@ def tile_list_tabgate_none_kernel(
         gather_scales(0, S)
         cast_w1(0, 0, 56)
         quantize_w1(0, 0, 4)
-        for c in range(4):
-            gather_words(0, 256 * c, 256 * (c + 1))
-        cast_w1(1, 0, 52)
-        quantize_w1(1, 0, 4)
+        gather_words(0, 0, 256)
+        gather_words(0, 256, 512)
+        gather_words(0, 512, 1024)
+        cast_part(1, 0, 2, 0, 96, True)
+        cast_part(1, 2, 4, 0, 128, False)
+        cast_part(1, 0, 2, 96, 128, False)
+        quantize_w1(1, 2, 4)
+        quantize_w1(1, 0, 2)
         for c in range(4):
             gather_words(1, 256 * c, 256 * (c + 1))
         for b in range(8):

@@ -196,8 +196,11 @@ def tile_list_tabgate_none_kernel(
             first_layer(1, b)
 
         gather_scales(0, S)
-        cast_w1(0, 0, 56)
-        quantize_w1(0, 0, 4)
+        cast_part(0, 0, 2, 0, 128, True)
+        cast_part(0, 2, 4, 0, 32, True)
+        cast_part(0, 2, 4, 32, 128, False)
+        quantize_w1(0, 0, 2)
+        quantize_w1(0, 2, 4)
         gather_words(0, 0, 256)
         gather_words(0, 256, 512)
         gather_words(0, 512, 1024)

@@ -18,7 +18,7 @@ MULT = mybir.AluOpType.mult
 
 P = 128
 BANK_TOKENS = 128
-RELU_ON_VECTOR = (3, 7)
+RELU_ON_VECTOR = (3,)
 W1_PIECES = (1, 1)
 
 
@@ -78,8 +78,10 @@ def tile_list_tabgate_none_kernel(
         def load_scale_quadrant(q, queue):
             queue.dma_start(table_scales[32 * q : 32 * q + 8, :], tab_scales[:, 4 * q : 4 * q + 4, :].bitcast(I32))
 
+        def load_w2_words():
+            nc.sync.dma_start(w2_codes[:].bitcast(I32), w2_words[0].bitcast(I32))
+
         def load_w2(queue):
-            queue.dma_start(w2_codes[:].bitcast(I32), w2_words[0].bitcast(I32))
             for q in range(4):
                 queue.dma_start(w2_sc[32 * q : 32 * q + 4, :], w2_scales[0, 4 * q : 4 * q + 4, :].bitcast(I32))
 
@@ -95,6 +97,7 @@ def tile_list_tabgate_none_kernel(
         load_w2(nc.sync)
         load_w1(1, 0)
         load_table(1)
+        load_w2_words()
         nc.sync.dma_start(gates[:], gT)
 
         def listed(lo, hi):
@@ -222,7 +225,6 @@ def tile_list_tabgate_none_kernel(
         relu(2)
         quantize_h(2, 4)
         acc1 = second_layer(2, 4)
-        relu(7)
         relu(4)
         copy_y(acc0, 0, 2)
         relu(5)
@@ -231,10 +233,13 @@ def tile_list_tabgate_none_kernel(
         gate_and_store(0, 2)
         relu(6)
         copy_y(acc1, 2, 4)
-        quantize_h(6, 8)
-        acc3 = second_layer(6, 8)
+        quantize_h(6, 7)
+        acc3 = second_layer(6, 7)
+        relu(7)
+        quantize_h(7, 8)
+        acc4 = second_layer(7, 8)
         copy_y(acc2, 4, 6)
         gate_and_store(2, 4)
         gate_and_store(4, 6)
-        mul_and_store(acc3[:, 0:128], 6, 7)
-        mul_and_store(acc3[:, 128:256], 7, 8)
+        mul_and_store(acc3[:], 6, 7)
+        mul_and_store(acc4[:], 7, 8)

@@ -90,7 +90,7 @@ def tile_list_tabgate_none_kernel(
 
         load_first_rows(0, 1)
         nc.sync.dma_start(offsets[:], offs)
-        for q in range(4):
+        for q in (2, 3, 0, 1):
             load_scale_quadrant(q, nc.sync)
         load_first_rows(1, 4)
         load_table(0)

@@ -41,9 +41,13 @@ def tile_list_tabgate_none_kernel(
             ]
             for a in range(2)
         ]
-        w1_bf = [keep.tile([P, 4, P, 4], BF16, name="w1_bf%d" % a, align_bytes=64) for a in range(2)]
-        w1_codes = [keep.tile([P, H], U32, name="w1_codes%d" % a, align_bytes=64) for a in range(2)]
-        w1_sc = [keep.tile([P, H], U8, name="w1_sc%d" % a, align_bytes=64) for a in range(2)]
+        w1_bf = keep.tile([P, 8, P, 4], BF16, name="w1_bf", align_bytes=64)
+        w1_codes = keep.tile([P, 2 * H], U32, name="w1_codes", align_bytes=64)
+        w1_sc = keep.tile([P, 2 * H], U8, name="w1_sc", align_bytes=64)
+
+        def place(a, t):
+            return t if a == 0 else 4 + (t + 2) % 4
+
         w2_codes = keep.tile([P, 2 * M], U8, name="w2_codes", align_bytes=64)
         w2_sc = keep.tile([P, M // 4], I32, name="w2_sc", align_bytes=64)
         v_codes = [keep.tile([P, S], U32, name="v_codes%d" % a, align_bytes=64) for a in range(2)]
@@ -109,27 +113,19 @@ def tile_list_tabgate_none_kernel(
         def gather_scales(lo, hi):
             nc.vector.tensor_copy(v_sc[:, lo:hi], table_scales[:].bitcast(U8).indirect(listed(lo, hi)))
 
-        def cast_w1(a, u, on_scalar):
-            width = P // W1_PIECES[a]
-            dst = w1_bf[a][:, :, width * u : width * (u + 1), :].rearrange("p t m j -> p m j t")
-            src = w1_raw[a][u][:].rearrange("p j (m t) -> p m j t", t=4)
-            nc.scalar.copy(dst[:, :on_scalar], src[:, :on_scalar])
-            if on_scalar < width:
-                nc.vector.tensor_copy(dst[:, on_scalar:], src[:, on_scalar:])
-
         def cast_part(a, t0, t1, m0, m1, on_scalar):
-            dst = w1_bf[a][:, t0:t1, m0:m1, :].rearrange("p t m j -> p m j t")
+            dst = w1_bf[:, place(a, t0) : place(a, t0) + t1 - t0, m0:m1, :].rearrange("p t m j -> p m j t")
             src = w1_raw[a][0][:].rearrange("p j (m t) -> p m j t", t=4)[:, m0:m1, :, t0:t1]
             if on_scalar:
                 nc.scalar.copy(dst, src)
             else:
                 nc.vector.tensor_copy(dst, src)
 
-        def quantize_w1(a, t0, t1):
+        def quantize_w1(t0, t1):
             nc.vector.quantize_mx(
-                out=w1_codes[a][:, P * t0 : P * t1].bitcast(FP8X4),
-                scales=w1_sc[a][:, P * t0 : P * t1],
-                in_=w1_bf[a][:, t0:t1, :, :].rearrange("p t m j -> p (t m j)"),
+                out=w1_codes[:, P * t0 : P * t1].bitcast(FP8X4),
+                scales=w1_sc[:, P * t0 : P * t1],
+                in_=w1_bf[:, t0:t1, :, :].rearrange("p t m j -> p (t m j)"),
             )
 
         banks = [psum.tile([P, 4, BANK_TOKENS], F32, name="bank%d" % b) for b in range(8)]
@@ -139,8 +135,8 @@ def tile_list_tabgate_none_kernel(
             for t in range(4):
                 nc.tensor.matmul_mx(
                     out=banks[b][:, t, :],
-                    lhsT=w1_codes[a][:, P * t : P * (t + 1)].bitcast(FP8X4),
-                    lhsT_scale=w1_sc[a][:, P * t : P * (t + 1)],
+                    lhsT=w1_codes[:, P * place(a, t) : P * (place(a, t) + 1)].bitcast(FP8X4),
+                    lhsT_scale=w1_sc[:, P * place(a, t) : P * (place(a, t) + 1)],
                     rhs=v_codes[a][:, cols].bitcast(FP8X4),
                     rhs_scale=v_sc[4 * a : P, cols],
                     start=(a == 0 and t == 0),
@@ -202,16 +198,17 @@ def tile_list_tabgate_none_kernel(
         cast_part(0, 0, 2, 0, 128, True)
         cast_part(0, 2, 4, 0, 32, True)
         cast_part(0, 2, 4, 32, 128, False)
-        quantize_w1(0, 0, 2)
-        quantize_w1(0, 2, 4)
+        quantize_w1(0, 2)
+        quantize_w1(2, 3)
         gather_words(0, 0, 256)
         gather_words(0, 256, 512)
         gather_words(0, 512, 1024)
         cast_part(1, 0, 2, 0, 96, True)
         cast_part(1, 2, 4, 0, 128, False)
         cast_part(1, 0, 2, 96, 128, False)
-        quantize_w1(1, 2, 4)
-        quantize_w1(1, 0, 2)
+        quantize_w1(3, 5)
+        quantize_w1(5, 6)
+        quantize_w1(6, 8)
         for c in range(4):
             gather_words(1, 256 * c, 256 * (c + 1))
         for b in range(8):

@@ -49,7 +49,6 @@ def tile_list_tabgate_none_kernel(
             return t if a == 0 else 4 + (t + 2) % 4
 
         w2_codes = keep.tile([P, 2 * M], U8, name="w2_codes", align_bytes=64)
-        w2_sc = keep.tile([P, M // 4], I32, name="w2_sc", align_bytes=64)
         v_codes = [keep.tile([P, S], U32, name="v_codes%d" % a, align_bytes=64) for a in range(2)]
         v_sc = keep.tile([P, S], U8, name="v_sc", align_bytes=64)
         h_bf = keep.tile([P, S, 4], BF16, name="h_bf", align_bytes=64)
@@ -61,7 +60,6 @@ def tile_list_tabgate_none_kernel(
         warm = keep.tile([P, 8], F32, name="warm")
 
         nc.vector.memset(table_scales[:], 0)
-        nc.vector.memset(w2_sc[:], 0)
         nc.vector.memset(warm[:], 0.0)
         nc.scalar.activation(warm[:, 0:1], warm[:, 1:2], RELU)
 
@@ -98,7 +96,6 @@ def tile_list_tabgate_none_kernel(
             load_scale_quadrant(q, nc.sync)
         load_first_rows(1, 4)
         load_table(0)
-        load_w2(nc.sync)
         load_w1(1, 0)
         load_table(1)
         load_w2_words()
@@ -198,6 +195,9 @@ def tile_list_tabgate_none_kernel(
         cast_part(0, 0, 2, 0, 128, True)
         cast_part(0, 2, 4, 0, 32, True)
         cast_part(0, 2, 4, 32, 128, False)
+        w2_sc = keep.tile([P, M // 4], I32, name="w1_raw00", align_bytes=64)
+        nc.vector.memset(w2_sc[:], 0)
+        load_w2(nc.scalar)
         quantize_w1(0, 2)
         quantize_w1(2, 3)
         gather_words(0, 0, 256)

@@ -203,9 +203,8 @@ def tile_list_tabgate_none_kernel(
         gather_words(0, 0, 256)
         gather_words(0, 256, 512)
         gather_words(0, 512, 1024)
-        cast_part(1, 0, 2, 0, 96, True)
+        cast_part(1, 0, 2, 0, 128, True)
         cast_part(1, 2, 4, 0, 128, False)
-        cast_part(1, 0, 2, 96, 128, False)
         quantize_w1(3, 5)
         quantize_w1(5, 6)
         quantize_w1(6, 8)

@@ -48,7 +48,6 @@ def tile_list_tabgate_none_kernel(
         def place(a, t):
             return t if a == 0 else 4 + (t + 2) % 4
 
-        w2_codes = keep.tile([P, 2 * M], U8, name="w2_codes", align_bytes=64)
         v_codes = [keep.tile([P, S], U32, name="v_codes%d" % a, align_bytes=64) for a in range(2)]
         v_sc = keep.tile([P, S], U8, name="v_sc", align_bytes=64)
         h_bf = keep.tile([P, S, 4], BF16, name="h_bf", align_bytes=64)
@@ -81,7 +80,7 @@ def tile_list_tabgate_none_kernel(
             queue.dma_start(table_scales[32 * q : 32 * q + 8, :], tab_scales[:, 4 * q : 4 * q + 4, :].bitcast(I32))
 
         def load_w2_words():
-            nc.sync.dma_start(w2_codes[:].bitcast(I32), w2_words[0].bitcast(I32))
+            nc.scalar.dma_start(w2_all[:, M // 4 :], w2_words[0].bitcast(I32))
 
         def load_w2(queue):
             for q in range(4):
@@ -98,7 +97,6 @@ def tile_list_tabgate_none_kernel(
         load_table(0)
         load_w1(1, 0)
         load_table(1)
-        load_w2_words()
         nc.sync.dma_start(gates[:], gT)
 
         def listed(lo, hi):
@@ -161,8 +159,8 @@ def tile_list_tabgate_none_kernel(
             acc = psum.tile([P, BANK_TOKENS * (b1 - b0)], F32, name="bank%d" % b0)
             nc.tensor.matmul_mx(
                 out=acc[:],
-                lhsT=w2_codes[:].bitcast(FP4X4),
-                lhsT_scale=w2_sc[:].bitcast(U8),
+                lhsT=w2_all[:, M // 4 :].bitcast(U8).bitcast(FP4X4),
+                lhsT_scale=w2_sc.bitcast(U8),
                 rhs=h_codes[:, cols].bitcast(FP8X4),
                 rhs_scale=h_sc[:, cols],
                 start=True,
@@ -195,18 +193,18 @@ def tile_list_tabgate_none_kernel(
         cast_part(0, 0, 2, 0, 128, True)
         cast_part(0, 2, 4, 0, 32, True)
         cast_part(0, 2, 4, 32, 128, False)
-        w2_sc = keep.tile([P, M // 4], I32, name="w1_raw00", align_bytes=64)
-        nc.vector.memset(w2_sc[:], 0)
+        w2_all = keep.tile([P, M // 4 + M // 2], I32, name="w1_raw00", align_bytes=64)
+        w2_sc = w2_all[:, 0 : M // 4]
+        nc.vector.memset(w2_sc, 0)
+        load_w2_words()
         load_w2(nc.scalar)
         quantize_w1(0, 2)
-        quantize_w1(2, 3)
         gather_words(0, 0, 256)
         gather_words(0, 256, 512)
         gather_words(0, 512, 1024)
         cast_part(1, 0, 2, 0, 128, True)
         cast_part(1, 2, 4, 0, 128, False)
-        quantize_w1(3, 5)
-        quantize_w1(5, 6)
+        quantize_w1(2, 6)
         quantize_w1(6, 8)
         for c in range(4):
             gather_words(1, 256 * c, 256 * (c + 1))

@@ -19,7 +19,6 @@ MULT = mybir.AluOpType.mult
 P = 128
 BANK_TOKENS = 128
 RELU_ON_VECTOR = (3,)
-W1_PIECES = (1, 1)
 
 
 def tile_list_tabgate_none_kernel(
@@ -31,16 +30,9 @@ def tile_list_tabgate_none_kernel(
         psum = ctx.enter_context(tc.psum_pool(name="psum", bufs=1))
 
         offsets = keep.tile([P, S // 16], U16, name="offsets")
-        table = [keep.tile([P, T], I32, name="table%d" % a, align_bytes=64) for a in range(2)]
-        table_scales = keep.tile([P, T // 4], I32, name="table_scales", align_bytes=64)
-        gates = keep.tile([P, T], F32, name="gates", align_bytes=64)
-        w1_raw = [
-            [
-                keep.tile([P, 4, H // W1_PIECES[a]], F32, name="w1_raw%d%d" % (a, u), align_bytes=64)
-                for u in range(W1_PIECES[a])
-            ]
-            for a in range(2)
-        ]
+        table_scales = keep.tile([P, T // 4], I32, name="table_scales", tag="slot_a", align_bytes=64)
+        w1_raw = {0: keep.tile([P, 4, H], F32, name="w1_raw0", tag="slot_b", align_bytes=64)}
+        table = {0: keep.tile([P, T], I32, name="table0", tag="slot_c", align_bytes=64)}
         w1_bf = keep.tile([P, 8, P, 4], BF16, name="w1_bf", align_bytes=64)
         w1_codes = keep.tile([P, 2 * H], U32, name="w1_codes", align_bytes=64)
         w1_sc = keep.tile([P, 2 * H], U8, name="w1_sc", align_bytes=64)
@@ -49,7 +41,8 @@ def tile_list_tabgate_none_kernel(
             return t if a == 0 else 4 + (t + 2) % 4
 
         v_codes = [keep.tile([P, S], U32, name="v_codes%d" % a, align_bytes=64) for a in range(2)]
-        v_sc = keep.tile([P, S], U8, name="v_sc", align_bytes=64)
+        v_rows = keep.tile([P, S], U8, name="v_rows", align_bytes=64)
+        v_sc = [keep.tile([P, S // 4], I32, name="v_sc%d" % a, align_bytes=64) for a in range(2)]
         h_bf = keep.tile([P, S, 4], BF16, name="h_bf", align_bytes=64)
         h_codes = keep.tile([P, S], U32, name="h_codes", align_bytes=64)
         h_sc = keep.tile([P, S], U8, name="h_sc", align_bytes=64)
@@ -58,46 +51,28 @@ def tile_list_tabgate_none_kernel(
         picked = keep.tile([P, S], F32, name="picked", align_bytes=64)
         warm = keep.tile([P, 8], F32, name="warm")
 
-        nc.vector.memset(table_scales[:], 0)
         nc.vector.memset(warm[:], 0.0)
         nc.scalar.activation(warm[:, 0:1], warm[:, 1:2], RELU)
+        nc.vector.memset(table_scales[32:64, :], 0)
+        nc.vector.memset(table_scales[64:128, :], 0)
+        nc.vector.memset(v_sc[0][:], 0)
+        nc.vector.memset(v_sc[1][:], 0)
 
         def load_table(a):
             nc.sync.dma_start(table[a][:], tab_words[a].rearrange("p t i -> p (t i)").bitcast(I32))
 
-        def load_w1(a, u):
-            rows = w1[512 * a : 512 * (a + 1), :].rearrange("(p j) c -> p j c", j=4)
-            nc.sync.dma_start(w1_raw[a][u][:], rows[:, :, H // W1_PIECES[a] * u : H // W1_PIECES[a] * (u + 1)])
+        def load_w1(a):
+            nc.sync.dma_start(w1_raw[a][:], w1[512 * a : 512 * (a + 1), :].rearrange("(p j) c -> p j c", j=4))
 
-        first_rows = w1[0:512, :].rearrange("(p j) c -> p j c", j=4)
-
-        def load_scale_rows(i):
-            a, q = i % 2, 2 * (i // 2 % 2) + i // 4
-            first = 32 * q + 4 * a
-            nc.sync.dma_start(table_scales[first : first + 4, :], tab_scales[a, 4 * q : 4 * q + 4, :].bitcast(I32))
-
-        def load_scale_quadrant(q, queue):
-            queue.dma_start(table_scales[32 * q : 32 * q + 8, :], tab_scales[:, 4 * q : 4 * q + 4, :].bitcast(I32))
-
-        def load_w2_words():
-            nc.scalar.dma_start(w2_all[:, M // 4 :], w2_words[0].bitcast(I32))
-
-        def load_w2(queue):
+        def move_scale_rows(a):
             for q in range(4):
-                queue.dma_start(w2_sc[32 * q : 32 * q + 4, :], w2_scales[0, 4 * q : 4 * q + 4, :].bitcast(I32))
+                first = 16 * a + 4 * q
+                nc.sync.dma_start(v_sc[a][32 * q : 32 * q + 4, :], v_rows[first : first + 4, :].bitcast(I32))
 
-        def load_first_rows(j0, j1):
-            nc.sync.dma_start(w1_raw[0][0][:, j0:j1, :], first_rows[:, j0:j1, :])
-
-        load_first_rows(0, 1)
+        nc.sync.dma_start(table_scales[0:32, :], tab_scales.rearrange("a q t -> (a q) t").bitcast(I32))
         nc.sync.dma_start(offsets[:], offs)
-        for q in (2, 3, 0, 1):
-            load_scale_quadrant(q, nc.sync)
-        load_first_rows(1, 4)
+        load_w1(0)
         load_table(0)
-        load_w1(1, 0)
-        load_table(1)
-        nc.sync.dma_start(gates[:], gT)
 
         def listed(lo, hi):
             return offsets[:, lo // 16 : hi // 16]
@@ -106,11 +81,11 @@ def tile_list_tabgate_none_kernel(
             nc.vector.tensor_copy(v_codes[a][:, lo:hi], table[a][:].bitcast(U32).indirect(listed(lo, hi)))
 
         def gather_scales(lo, hi):
-            nc.vector.tensor_copy(v_sc[:, lo:hi], table_scales[:].bitcast(U8).indirect(listed(lo, hi)))
+            nc.vector.tensor_copy(v_rows[:, lo:hi], table_scales[:].bitcast(U8).indirect(listed(lo, hi)))
 
         def cast_part(a, t0, t1, m0, m1, on_scalar):
             dst = w1_bf[:, place(a, t0) : place(a, t0) + t1 - t0, m0:m1, :].rearrange("p t m j -> p m j t")
-            src = w1_raw[a][0][:].rearrange("p j (m t) -> p m j t", t=4)[:, m0:m1, :, t0:t1]
+            src = w1_raw[a][:].rearrange("p j (m t) -> p m j t", t=4)[:, m0:m1, :, t0:t1]
             if on_scalar:
                 nc.scalar.copy(dst, src)
             else:
@@ -133,7 +108,7 @@ def tile_list_tabgate_none_kernel(
                     lhsT=w1_codes[:, P * place(a, t) : P * (place(a, t) + 1)].bitcast(FP8X4),
                     lhsT_scale=w1_sc[:, P * place(a, t) : P * (place(a, t) + 1)],
                     rhs=v_codes[a][:, cols].bitcast(FP8X4),
-                    rhs_scale=v_sc[4 * a : P, cols],
+                    rhs_scale=v_sc[a][:].bitcast(U8)[:, cols],
                     start=(a == 0 and t == 0),
                     stop=(a == 1 and t == 3),
                 )
@@ -190,20 +165,29 @@ def tile_list_tabgate_none_kernel(
             first_layer(1, b)
 
         gather_scales(0, S)
+        move_scale_rows(0)
+        w1_raw[1] = keep.tile([P, 4, H], F32, name="w1_raw1", tag="slot_a", align_bytes=64)
+        load_w1(1)
+        move_scale_rows(1)
         cast_part(0, 0, 2, 0, 128, True)
         cast_part(0, 2, 4, 0, 32, True)
         cast_part(0, 2, 4, 32, 128, False)
-        w2_all = keep.tile([P, M // 4 + M // 2], I32, name="w1_raw00", align_bytes=64)
-        w2_sc = w2_all[:, 0 : M // 4]
-        nc.vector.memset(w2_sc, 0)
-        load_w2_words()
-        load_w2(nc.scalar)
+        table[1] = keep.tile([P, T], I32, name="table1", tag="slot_b", align_bytes=64)
+        load_table(1)
         quantize_w1(0, 2)
         gather_words(0, 0, 256)
         gather_words(0, 256, 512)
         gather_words(0, 512, 1024)
+        gates = keep.tile([P, T], F32, name="gates", tag="slot_c", align_bytes=64)
+        nc.sync.dma_start(gates[:], gT)
         cast_part(1, 0, 2, 0, 128, True)
         cast_part(1, 2, 4, 0, 128, False)
+        w2_all = keep.tile([P, M // 4 + M // 2], I32, name="w2_all", tag="slot_a", align_bytes=64)
+        w2_sc = w2_all[:, 0 : M // 4]
+        nc.gpsimd.memset(w2_sc, 0)
+        nc.scalar.dma_start(w2_all[:, M // 4 :], w2_words[0].bitcast(I32))
+        for q in range(4):
+            nc.scalar.dma_start(w2_sc[32 * q : 32 * q + 4, :], w2_scales[0, 4 * q : 4 * q + 4, :].bitcast(I32))
         quantize_w1(2, 6)
         quantize_w1(6, 8)
         for c in range(4):

@@ -56,7 +56,6 @@ def tile_list_tabgate_none_kernel(
         nc.vector.memset(table_scales[32:64, :], 0)
         nc.vector.memset(table_scales[64:128, :], 0)
         nc.vector.memset(v_sc[0][:], 0)
-        nc.vector.memset(v_sc[1][:], 0)
 
         def load_table(a):
             nc.sync.dma_start(table[a][:], tab_words[a].rearrange("p t i -> p (t i)").bitcast(I32))
@@ -65,7 +64,7 @@ def tile_list_tabgate_none_kernel(
             nc.sync.dma_start(w1_raw[a][:], w1[512 * a : 512 * (a + 1), :].rearrange("(p j) c -> p j c", j=4))
 
         def move_scale_rows(a):
-            for q in range(4):
+            for q in range(1 - a, 4):
                 first = 16 * a + 4 * q
                 nc.sync.dma_start(v_sc[a][32 * q : 32 * q + 4, :], v_rows[first : first + 4, :].bitcast(I32))
 
@@ -166,12 +165,14 @@ def tile_list_tabgate_none_kernel(
 
         gather_scales(0, S)
         move_scale_rows(0)
+        nc.vector.tensor_copy(v_sc[0][0:32, :], v_rows[0:32, :].bitcast(I32))
         w1_raw[1] = keep.tile([P, 4, H], F32, name="w1_raw1", tag="slot_a", align_bytes=64)
         load_w1(1)
-        move_scale_rows(1)
         cast_part(0, 0, 2, 0, 128, True)
         cast_part(0, 2, 4, 0, 32, True)
         cast_part(0, 2, 4, 32, 128, False)
+        nc.vector.tensor_copy(v_sc[1][:], v_rows[:].bitcast(I32))
+        move_scale_rows(1)
         table[1] = keep.tile([P, T], I32, name="table1", tag="slot_b", align_bytes=64)
         load_table(1)
         quantize_w1(0, 2)

@@ -19,6 +19,7 @@ MULT = mybir.AluOpType.mult
 P = 128
 BANK_TOKENS = 128
 RELU_ON_VECTOR = (3,)
+PLANE_ROW = (12, 0)
 
 
 def tile_list_tabgate_none_kernel(
@@ -51,11 +52,10 @@ def tile_list_tabgate_none_kernel(
         picked = keep.tile([P, S], F32, name="picked", align_bytes=64)
         warm = keep.tile([P, 8], F32, name="warm")
 
-        nc.vector.memset(warm[:], 0.0)
+        nc.vector.memset(table_scales[0:96, :], 0)
+        nc.gpsimd.memset(warm[:], 0.0)
         nc.scalar.activation(warm[:, 0:1], warm[:, 1:2], RELU)
-        nc.vector.memset(table_scales[32:64, :], 0)
-        nc.vector.memset(table_scales[64:128, :], 0)
-        nc.vector.memset(v_sc[0][:], 0)
+        nc.gpsimd.memset(v_sc[0][0:96, :], 0)
 
         def load_table(a):
             nc.sync.dma_start(table[a][:], tab_words[a].rearrange("p t i -> p (t i)").bitcast(I32))
@@ -64,11 +64,12 @@ def tile_list_tabgate_none_kernel(
             nc.sync.dma_start(w1_raw[a][:], w1[512 * a : 512 * (a + 1), :].rearrange("(p j) c -> p j c", j=4))
 
         def move_scale_rows(a):
-            for q in range(1 - a, 4):
-                first = 16 * a + 4 * q
-                nc.sync.dma_start(v_sc[a][32 * q : 32 * q + 4, :], v_rows[first : first + 4, :].bitcast(I32))
+            for q in range(3 + a):
+                first = 96 + 16 * a + 4 * q
+                want = 32 * q + PLANE_ROW[a]
+                nc.sync.dma_start(v_sc[a][want : want + 4, :], v_rows[first : first + 4, :].bitcast(I32))
 
-        nc.sync.dma_start(table_scales[0:32, :], tab_scales.rearrange("a q t -> (a q) t").bitcast(I32))
+        nc.sync.dma_start(table_scales[96:128, :], tab_scales.rearrange("a q t -> (a q) t").bitcast(I32))
         nc.sync.dma_start(offsets[:], offs)
         load_w1(0)
         load_table(0)
@@ -107,7 +108,7 @@ def tile_list_tabgate_none_kernel(
                     lhsT=w1_codes[:, P * place(a, t) : P * (place(a, t) + 1)].bitcast(FP8X4),
                     lhsT_scale=w1_sc[:, P * place(a, t) : P * (place(a, t) + 1)],
                     rhs=v_codes[a][:, cols].bitcast(FP8X4),
-                    rhs_scale=v_sc[a][:].bitcast(U8)[:, cols],
+                    rhs_scale=v_sc[a][:].bitcast(U8)[PLANE_ROW[a] : P, cols],
                     start=(a == 0 and t == 0),
                     stop=(a == 1 and t == 3),
                 )
@@ -165,7 +166,7 @@ def tile_list_tabgate_none_kernel(
 
         gather_scales(0, S)
         move_scale_rows(0)
-        nc.vector.tensor_copy(v_sc[0][0:32, :], v_rows[0:32, :].bitcast(I32))
+        nc.vector.tensor_copy(v_sc[0][96:128, :], v_rows[96:128, :].bitcast(I32))
         w1_raw[1] = keep.tile([P, 4, H], F32, name="w1_raw1", tag="slot_a", align_bytes=64)
         load_w1(1)
         cast_part(0, 0, 2, 0, 128, True)

@@ -177,6 +177,7 @@ def tile_list_tabgate_none_kernel(
         table[1] = keep.tile([P, T], I32, name="table1", tag="slot_b", align_bytes=64)
         load_table(1)
         quantize_w1(0, 2)
+        quantize_w1(2, 3)
         gather_words(0, 0, 256)
         gather_words(0, 256, 512)
         gather_words(0, 512, 1024)
@@ -190,7 +191,8 @@ def tile_list_tabgate_none_kernel(
         nc.scalar.dma_start(w2_all[:, M // 4 :], w2_words[0].bitcast(I32))
         for q in range(4):
             nc.scalar.dma_start(w2_sc[32 * q : 32 * q + 4, :], w2_scales[0, 4 * q : 4 * q + 4, :].bitcast(I32))
-        quantize_w1(2, 6)
+        quantize_w1(3, 5)
+        quantize_w1(5, 6)
         quantize_w1(6, 8)
         for c in range(4):
             gather_words(1, 256 * c, 256 * (c + 1))

@@ -194,8 +194,8 @@ def tile_list_tabgate_none_kernel(
         quantize_w1(3, 5)
         quantize_w1(5, 6)
         quantize_w1(6, 8)
-        for c in range(4):
-            gather_words(1, 256 * c, 256 * (c + 1))
+        for lo, hi in ((0, 128), (128, 384), (384, 640), (640, 1024)):
+            gather_words(1, lo, hi)
         for b in range(8):
             both_passes(b)
         relu(0)

@@ -63,11 +63,14 @@ def tile_list_tabgate_none_kernel(
         def load_w1(a):
             nc.sync.dma_start(w1_raw[a][:], w1[512 * a : 512 * (a + 1), :].rearrange("(p j) c -> p j c", j=4))
 
-        def move_scale_rows(a):
-            for q in range(3 + a):
-                first = 96 + 16 * a + 4 * q
-                want = 32 * q + PLANE_ROW[a]
-                nc.sync.dma_start(v_sc[a][want : want + 4, :], v_rows[first : first + 4, :].bitcast(I32))
+        def move_quadrants():
+            for q in range(3):
+                src = v_rows[96 + 4 * q : 100 + 4 * q, :].bitcast(I32)
+                nc.sync.dma_start(v_sc[0][32 * q + 12 : 32 * q + 16, :], src)
+
+        def move_rows():
+            for r in range(4):
+                nc.sync.dma_start(v_sc[1][r:P:32, :], v_rows[112 + r : P : 4, :].bitcast(I32))
 
         nc.sync.dma_start(table_scales[96:128, :], tab_scales.rearrange("a q t -> (a q) t").bitcast(I32))
         nc.sync.dma_start(offsets[:], offs)
@@ -165,7 +168,7 @@ def tile_list_tabgate_none_kernel(
             first_layer(1, b)
 
         gather_scales(0, S)
-        move_scale_rows(0)
+        move_quadrants()
         nc.vector.tensor_copy(v_sc[0][96:128, :], v_rows[96:128, :].bitcast(I32))
         w1_raw[1] = keep.tile([P, 4, H], F32, name="w1_raw1", tag="slot_a", align_bytes=64)
         load_w1(1)
@@ -173,7 +176,7 @@ def tile_list_tabgate_none_kernel(
         cast_part(0, 2, 4, 0, 32, True)
         cast_part(0, 2, 4, 32, 128, False)
         nc.vector.tensor_copy(v_sc[1][:], v_rows[:].bitcast(I32))
-        move_scale_rows(1)
+        move_rows()
         table[1] = keep.tile([P, T], I32, name="table1", tag="slot_b", align_bytes=64)
         load_table(1)
         quantize_w1(0, 2)

from contextlib import ExitStack

import concourse.mybir as mybir

K, M, T, S, H = 1024, 128, 2048, 1024, 512
FLOPS = 2 * K * H * S + 2 * H * M * S

F32 = mybir.dt.float32
BF16 = mybir.dt.bfloat16
I32 = mybir.dt.int32
U32 = mybir.dt.uint32
U16 = mybir.dt.uint16
U8 = mybir.dt.uint8
FP8X4 = mybir.dt.float8_e4m3fn_x4
FP4X4 = mybir.dt.float4_e2m1fn_x4
RELU = mybir.ActivationFunctionType.Relu
MULT = mybir.AluOpType.mult

P = 128
BANK_TOKENS = 128
RELU_ON_VECTOR = (3,)
PLANE_ROW = (12, 0)


def tile_list_tabgate_none_kernel(
    tc, tab_words, tab_scales, w1, w2_words, w2_scales, gT, offs, out
):
    nc = tc.nc
    with ExitStack() as ctx:
        keep = ctx.enter_context(tc.tile_pool(name="keep", bufs=1))
        psum = ctx.enter_context(tc.psum_pool(name="psum", bufs=1))

        offsets = keep.tile([P, S // 16], U16, name="offsets")
        table_scales = keep.tile([P, T // 4], I32, name="table_scales", tag="slot_a", align_bytes=64)
        w1_raw = {0: keep.tile([P, 4, H], F32, name="w1_raw0", tag="slot_b", align_bytes=64)}
        table = {0: keep.tile([P, T], I32, name="table0", tag="slot_c", align_bytes=64)}
        w1_bf = keep.tile([P, 8, P, 4], BF16, name="w1_bf", align_bytes=64)
        w1_codes = keep.tile([P, 2 * H], U32, name="w1_codes", align_bytes=64)
        w1_sc = keep.tile([P, 2 * H], U8, name="w1_sc", align_bytes=64)

        def place(a, t):
            return t if a == 0 else 4 + (t + 2) % 4

        v_codes = [keep.tile([P, S], U32, name="v_codes%d" % a, align_bytes=64) for a in range(2)]
        v_rows = keep.tile([P, S], U8, name="v_rows", align_bytes=64)
        v_sc = [keep.tile([P, S // 4], I32, name="v_sc%d" % a, align_bytes=64) for a in range(2)]
        h_bf = keep.tile([P, S, 4], BF16, name="h_bf", align_bytes=64)
        h_codes = keep.tile([P, S], U32, name="h_codes", align_bytes=64)
        h_sc = keep.tile([P, S], U8, name="h_sc", align_bytes=64)
        y = keep.tile([P, S], F32, name="y", align_bytes=64)
        result = keep.tile([P, S], F32, name="result", align_bytes=64)
        picked = keep.tile([P, S], F32, name="picked", align_bytes=64)
        warm = keep.tile([P, 8], F32, name="warm")

        nc.vector.memset(table_scales[0:96, :], 0)
        nc.gpsimd.memset(warm[:], 0.0)
        nc.scalar.activation(warm[:, 0:1], warm[:, 1:2], RELU)
        nc.gpsimd.memset(v_sc[0][0:96, :], 0)

        def load_table(a):
            nc.sync.dma_start(table[a][:], tab_words[a].rearrange("p t i -> p (t i)").bitcast(I32))

        def load_w1(a):
            nc.sync.dma_start(w1_raw[a][:], w1[512 * a : 512 * (a + 1), :].rearrange("(p j) c -> p j c", j=4))

        def move_quadrants():
            for q in range(3):
                src = v_rows[96 + 4 * q : 100 + 4 * q, :].bitcast(I32)
                nc.sync.dma_start(v_sc[0][32 * q + 12 : 32 * q + 16, :], src)

        def move_rows():
            for r in range(4):
                nc.sync.dma_start(v_sc[1][r:P:32, :], v_rows[112 + r : P : 4, :].bitcast(I32))

        nc.sync.dma_start(table_scales[96:128, :], tab_scales.rearrange("a q t -> (a q) t").bitcast(I32))
        nc.sync.dma_start(offsets[:], offs)
        load_w1(0)
        load_table(0)

        def listed(lo, hi):
            return offsets[:, lo // 16 : hi // 16]

        def gather_words(a, lo, hi):
            nc.vector.tensor_copy(v_codes[a][:, lo:hi], table[a][:].bitcast(U32).indirect(listed(lo, hi)))

        def gather_scales(lo, hi):
            nc.vector.tensor_copy(v_rows[:, lo:hi], table_scales[:].bitcast(U8).indirect(listed(lo, hi)))

        def cast_part(a, t0, t1, m0, m1, on_scalar):
            dst = w1_bf[:, place(a, t0) : place(a, t0) + t1 - t0, m0:m1, :].rearrange("p t m j -> p m j t")
            src = w1_raw[a][:].rearrange("p j (m t) -> p m j t", t=4)[:, m0:m1, :, t0:t1]
            if on_scalar:
                nc.scalar.copy(dst, src)
            else:
                nc.vector.tensor_copy(dst, src)

        def quantize_w1(t0, t1):
            nc.vector.quantize_mx(
                out=w1_codes[:, P * t0 : P * t1].bitcast(FP8X4),
                scales=w1_sc[:, P * t0 : P * t1],
                in_=w1_bf[:, t0:t1, :, :].rearrange("p t m j -> p (t m j)"),
            )

        banks = [psum.tile([P, 4, BANK_TOKENS], F32, name="bank%d" % b) for b in range(8)]

        def first_layer(a, b):
            cols = slice(BANK_TOKENS * b, BANK_TOKENS * (b + 1))
            for t in range(4):
                nc.tensor.matmul_mx(
                    out=banks[b][:, t, :],
                    lhsT=w1_codes[:, P * place(a, t) : P * (place(a, t) + 1)].bitcast(FP8X4),
                    lhsT_scale=w1_sc[:, P * place(a, t) : P * (place(a, t) + 1)],
                    rhs=v_codes[a][:, cols].bitcast(FP8X4),
                    rhs_scale=v_sc[a][:].bitcast(U8)[PLANE_ROW[a] : P, cols],
                    start=(a == 0 and t == 0),
                    stop=(a == 1 and t == 3),
                )

        def relu(b):
            cols = slice(BANK_TOKENS * b, BANK_TOKENS * (b + 1))
            src = banks[b][:].rearrange("p t n -> p n t")
            if b in RELU_ON_VECTOR:
                nc.vector.tensor_scalar_max(h_bf[:, cols, :], src, 0.0)
            else:
                nc.scalar.activation(h_bf[:, cols, :], src, RELU)

        def quantize_h(b0, b1):
            cols = slice(BANK_TOKENS * b0, BANK_TOKENS * b1)
            nc.vector.quantize_mx(
                out=h_codes[:, cols].bitcast(FP8X4),
                scales=h_sc[:, cols],
                in_=h_bf[:, cols, :].rearrange("p n t -> p (n t)"),
            )

        def second_layer(b0, b1):
            cols = slice(BANK_TOKENS * b0, BANK_TOKENS * b1)
            acc = psum.tile([P, BANK_TOKENS * (b1 - b0)], F32, name="bank%d" % b0)
            nc.tensor.matmul_mx(
                out=acc[:],
                lhsT=w2_all[:, M // 4 :].bitcast(U8).bitcast(FP4X4),
                lhsT_scale=w2_sc.bitcast(U8),
                rhs=h_codes[:, cols].bitcast(FP8X4),
                rhs_scale=h_sc[:, cols],
                start=True,
                stop=True,
            )
            return acc

        def gate_and_store(b0, b1):
            lo, hi = BANK_TOKENS * b0, BANK_TOKENS * b1
            nc.vector.tensor_tensor(result[:, lo:hi], gates[:].indirect(listed(lo, hi)), y[:, lo:hi], MULT)
            nc.sync.dma_start(out[:, lo:hi], result[:, lo:hi])

        def copy_y(acc, b0, b1):
            nc.scalar.copy(y[:, BANK_TOKENS * b0 : BANK_TOKENS * b1], acc[:])

        def pick_gates(b0, b1):
            lo, hi = BANK_TOKENS * b0, BANK_TOKENS * b1
            nc.vector.tensor_copy(picked[:, lo:hi], gates[:].indirect(listed(lo, hi)))

        def mul_and_store(acc, b0, b1):
            lo, hi = BANK_TOKENS * b0, BANK_TOKENS * b1
            nc.vector.tensor_tensor(result[:, lo:hi], acc, picked[:, lo:hi], MULT)
            nc.sync.dma_start(out[:, lo:hi], result[:, lo:hi])

        def both_passes(b):
            first_layer(0, b)
            first_layer(1, b)

        gather_scales(0, S)
        move_quadrants()
        nc.vector.tensor_copy(v_sc[0][96:128, :], v_rows[96:128, :].bitcast(I32))
        w1_raw[1] = keep.tile([P, 4, H], F32, name="w1_raw1", tag="slot_a", align_bytes=64)
        load_w1(1)
        cast_part(0, 0, 2, 0, 128, True)
        cast_part(0, 2, 4, 0, 32, True)
        cast_part(0, 2, 4, 32, 128, False)
        nc.vector.tensor_copy(v_sc[1][:], v_rows[:].bitcast(I32))
        move_rows()
        table[1] = keep.tile([P, T], I32, name="table1", tag="slot_b", align_bytes=64)
        load_table(1)
        quantize_w1(0, 2)
        quantize_w1(2, 3)
        gather_words(0, 0, 256)
        gather_words(0, 256, 512)
        gather_words(0, 512, 1024)
        gates = keep.tile([P, T], F32, name="gates", tag="slot_c", align_bytes=64)
        nc.sync.dma_start(gates[:], gT)
        cast_part(1, 0, 2, 0, 128, True)
        cast_part(1, 2, 4, 0, 128, False)
        w2_all = keep.tile([P, M // 4 + M // 2], I32, name="w2_all", tag="slot_a", align_bytes=64)
        w2_sc = w2_all[:, 0 : M // 4]
        nc.gpsimd.memset(w2_sc, 0)
        nc.scalar.dma_start(w2_all[:, M // 4 :], w2_words[0].bitcast(I32))
        for q in range(4):
            nc.scalar.dma_start(w2_sc[32 * q : 32 * q + 4, :], w2_scales[0, 4 * q : 4 * q + 4, :].bitcast(I32))
        quantize_w1(3, 5)
        quantize_w1(5, 6)
        quantize_w1(6, 8)
        for lo, hi in ((0, 128), (128, 384), (384, 640), (640, 1024)):
            gather_words(1, lo, hi)
        for b in range(8):
            both_passes(b)
        relu(0)
        relu(1)
        relu(3)
        pick_gates(6, 8)
        quantize_h(0, 2)
        acc0 = second_layer(0, 2)
        relu(2)
        quantize_h(2, 4)
        acc1 = second_layer(2, 4)
        relu(4)
        copy_y(acc0, 0, 2)
        relu(5)
        quantize_h(4, 6)
        acc2 = second_layer(4, 6)
        gate_and_store(0, 2)
        relu(6)
        copy_y(acc1, 2, 4)
        quantize_h(6, 7)
        acc3 = second_layer(6, 7)
        relu(7)
        quantize_h(7, 8)
        acc4 = second_layer(7, 8)
        copy_y(acc2, 4, 6)
        gate_and_store(2, 4)
        gate_and_store(4, 6)
        mul_and_store(acc3[:], 6, 7)
        mul_and_store(acc4[:], 7, 8)
